import numpy as np
import ml_dtypes


def mxq(x, axis, fmt="e4m3"):
    dtype, down = {"e4m3": (ml_dtypes.float8_e4m3fn, 7), "e5m2": (ml_dtypes.float8_e5m2, 14)}[fmt]
    v = np.moveaxis(np.asarray(x, np.float32).astype(ml_dtypes.bfloat16).astype(np.float64), axis, -1)
    blocks = v.reshape(v.shape[:-1] + (-1, 32))
    amax = np.abs(blocks).max(-1, keepdims=True)
    byte = np.maximum(np.where(amax > 0, np.frexp(amax)[1] - 1 + 127, 0) - down, 1)
    scale = np.exp2(byte - 127.0)
    codes = (blocks / scale).astype(np.float32).astype(dtype).astype(np.float64)
    return np.moveaxis((codes * scale).reshape(v.shape), -1, axis)


WIDE = False


def mx_kscale(k):
    if not WIDE:
        return np.ones(k)
    levels = np.array([10, -10, 5, -5, 0])
    if k % 512:
        return np.exp2(np.random.permutation(np.resize(levels, k // 32))).repeat(32)
    a = np.empty((k // 512, 16))
    for p in range(k // 512):
        a[p, :8] = np.random.permutation(np.resize(levels, 8))
        for g in range(8):
            far = levels[np.abs(levels - a[p, g]) >= 10]
            a[p, g + 8] = far[np.random.randint(len(far))]
    return np.exp2(a.ravel()).repeat(32)


def f64(x):
    return np.asarray(x).astype(np.float64)


def striped(idx):
    return np.tile(idx.reshape(-1, 16).T, (8, 1)).astype(np.uint16)


def unstriped(offs):
    return offs[:16].T.reshape(-1).astype(np.int64)


def relu(v):
    return np.maximum(v, 0.0)


K, T, E, C, N = 1024, 1024, 16, 128, 128


def by_expert(wq, xq):
    return np.concatenate([wq[e].T @ xq[:, e * C:(e + 1) * C] for e in range(E)], axis=1)


def setup_inputs():
    n = np.random.standard_normal
    s = mx_kscale(K)[:, None]
    first = np.random.permutation(np.repeat(np.arange(E), T // E))
    second = (first + 1 + np.random.permutation(np.repeat(np.arange(E - 1), -(-T // (E - 1)))[:T])) % E
    while np.bincount(second, minlength=E).max() != T // E:
        load = np.bincount(second, minlength=E); hi, lo = int(load.argmax()), int(load.argmin())
        t = np.flatnonzero((second == hi) & (first != lo))[0]; second[t] = lo
    slot_token = np.empty(E * C, np.int64); pos = np.empty((2, T), np.int64); fill = np.zeros(E, np.int64)
    place = np.stack([np.random.permutation(C) for _ in range(E)])
    for r, deal in enumerate((first, second)):
        for t in np.random.permutation(T):
            e = deal[t]; j = e * C + place[e, fill[e]]; fill[e] += 1; slot_token[j] = t; pos[r, t] = j
    g = np.random.uniform(0.2, 0.8, T)
    return {
        "xT": (n((K, T)) * s).astype(np.float32),
        "w": (n((E, K, N)) / np.sqrt(K) / s[None]).astype(np.float32),
        "b": (0.3 * n((N, E))).astype(np.float32),
        "gate": np.stack([np.tile(g, (N, 1)), np.tile(1.0 - g, (N, 1))]).astype(np.float32),
        "offs": striped(slot_token),
        "pos1": striped(pos[0]),
        "pos2": striped(pos[1]),
    }


def reference(xT, w, b, gate, offs, pos1, pos2):
    idx = unstriped(offs)
    xq = mxq(f64(xT)[:, idx], 0, "e4m3")
    y = by_expert(mxq(f64(w), 1, "e4m3"), xq)
    y = relu(y + np.repeat(f64(b), C, axis=1))
    return f64(gate[0]) * y[:, unstriped(pos1)] + f64(gate[1]) * y[:, unstriped(pos2)]

@@ -1,0 +1,175 @@
+from contextlib import ExitStack
+
+import concourse.mybir as mybir
+
+K, T, E, C, N = 1024, 1024, 16, 128, 128
+FLOPS = 2 * K * N * E * C
+
+F32 = mybir.dt.float32
+BF16 = mybir.dt.bfloat16
+U32 = mybir.dt.uint32
+I32 = mybir.dt.int32
+U16 = mybir.dt.uint16
+U8 = mybir.dt.uint8
+FP8X4 = mybir.dt.float8_e4m3fn_x4
+MULT = mybir.AluOpType.mult
+ADD = mybir.AluOpType.add
+RELU = mybir.ActivationFunctionType.Relu
+
+P = 128
+PACK = 4
+PASSES = K // (P * PACK)
+WINDOW = 2 * T
+X_LOADS = (((0, 512), (512, 768), (768, 1024)), ((0, 512), (512, 1024)))
+X_BATCHES = (((0, 512), (512, 768), (768, 1024)), ((0, 512), (512, 1024)))
+V_PART = 5
+W_LOADS = ((0, 4), (4, 8), (8, 12), (12, 16), (16, 20), (20, 24), (24, 26), (26, 28), (28, 30), (30, 31), (31, 32))
+W_BATCHES = ((0, 4), (4, 8), (8, 12), (12, 16), (16, 20), (20, 24), (24, 26), (26, 28), (28, 30), (30, 31), (31, 32))
+SLICES = ((0, 12), (12, 16))
+VECTOR_LOADS = (7, 8, 9, 10)
+LAST_SCALAR_LOAD = 6
+BANKS = ((0, 4), (4, 6), (6, 8), (8, 10), (10, 12), (12, 14), (14, 15), (15, 16))
+
+
+def find(ranges, i):
+    return [k for k, (r0, r1) in enumerate(ranges) if r0 <= i < r1][0]
+
+
+def tile_routed_moe_kernel(tc, xT, w, b, gate, offs, pos1, pos2, out):
+    nc = tc.nc
+    with ExitStack() as ctx:
+        lists = ctx.enter_context(tc.tile_pool(name="lists", bufs=1))
+        keep = ctx.enter_context(tc.tile_pool(name="keep", bufs=1))
+        psum = ctx.enter_context(tc.psum_pool(name="psum", bufs=1))
+
+        offs_sb = lists.tile([P, E * C // 16], U16, name="offs_sb")
+        pos1_sb = lists.tile([P, T // 16], U16, name="pos1_sb")
+        pos2_sb = lists.tile([P, T // 16], U16, name="pos2_sb")
+
+        x_raw = [[keep.tile([P, PACK, t1 - t0], F32, name="x_raw%d%d" % (a, i)) for i, (t0, t1) in enumerate(X_LOADS[a])] for a in range(PASSES)]
+        x_grp = [[keep.tile([P, t1 - t0, PACK], BF16, name="x_grp%d%d" % (a, i), align_bytes=64) for i, (t0, t1) in enumerate(X_BATCHES[a])] for a in range(PASSES)]
+        x_codes = [keep.tile([P, WINDOW], I32, name="x_codes%d" % a, align_bytes=64) for a in range(PASSES)]
+        x_scales = keep.tile([P, WINDOW], U8, name="x_scales", align_bytes=64)
+        w_raw = [keep.tile([P, g1 - g0, PACK * N], F32, name="w_raw%d" % c, tag="raw%d" % c) for c, (g0, g1) in enumerate(W_LOADS)]
+        w_grp = [keep.tile([P, g1 - g0, N, PACK], BF16, name="w_grp%d" % q, tag="slot%d" % q, align_bytes=64) for q, (g0, g1) in enumerate(W_BATCHES)]
+        w_codes = [keep.tile([P, (g1 - g0) * N], U32, name="w_codes%d" % q, align_bytes=64) for q, (g0, g1) in enumerate(W_BATCHES)]
+        w_scales = [keep.tile([P, (g1 - g0) * N], U8, name="w_scales%d" % q, align_bytes=64) for q, (g0, g1) in enumerate(W_BATCHES)]
+        b_sb = keep.tile([P, E], F32, name="b_sb")
+        gate_sb = keep.tile([P, 2, T], F32, name="gate_sb")
+        y = keep.tile([P, E * C], F32, name="y")
+        acc = [psum.tile([N, e1 - e0, C], F32, name="acc%d" % k) for k, (e0, e1) in enumerate(BANKS)]
+        g_codes = {}
+        g_scales = {}
+
+        x_view = xT.rearrange("(a p j) t -> a p j t", a=PASSES, p=P, j=PACK)
+        w_view = w.rearrange("e (a p j) n -> p (e a) (j n)", a=PASSES, p=P, j=PACK)
+        nc.sync.dma_start(offs_sb[:], offs)
+        for a in range(PASSES):
+            for i, (t0, t1) in enumerate(X_LOADS[a]):
+                nc.sync.dma_start(x_raw[a][i][:], x_view[a][:, :, t0:t1])
+        for c, (g0, g1) in enumerate(W_LOADS):
+            nc.sync.dma_start(w_raw[c][:], w_view[:, g0:g1, :])
+            if c == LAST_SCALAR_LOAD:
+                nc.sync.dma_start(b_sb[:], b)
+        nc.sync.dma_start(pos1_sb[:], pos1)
+        nc.sync.dma_start(pos2_sb[:], pos2)
+        for g in range(2):
+            nc.sync.dma_start(gate_sb[:, g, :], gate[g])
+
+        nc.vector.memset(x_scales[:].bitcast(I32), 0)
+        for a in range(PASSES):
+            nc.vector.memset(x_codes[a][:, T:WINDOW], 0)
+
+        def interleave_x(copy, a, i, t0, t1):
+            base = X_LOADS[a][i][0]
+            q = find(X_BATCHES[a], base + t0)
+            shift = base - X_BATCHES[a][q][0]
+            copy(
+                out=x_grp[a][q][:, shift + t0:shift + t1, :].rearrange("p (c i) j -> p c j i", i=4),
+                in_=x_raw[a][i][:, :, t0:t1].rearrange("p j (c i) -> p c j i", i=4),
+            )
+
+        def quantize_x(a, q):
+            t0, t1 = X_BATCHES[a][q]
+            nc.vector.quantize_mx(
+                out=x_codes[a][:, t0:t1].bitcast(FP8X4),
+                scales=x_scales[PACK * a:P, t0:t1],
+                in_=x_grp[a][q][:].rearrange("p t j -> p (t j)"),
+            )
+
+        def gather_codes(a, s, tag):
+            e0, e1 = SLICES[s]
+            g_codes[(a, s)] = keep.tile([P, (e1 - e0) * C], U32, name="g_codes%d%d" % (a, s), tag=tag, align_bytes=64)
+            nc.vector.tensor_copy(out=g_codes[(a, s)][:], in_=x_codes[a][:].bitcast(U32).indirect(offs_sb[:, e0 * C // 16:e1 * C // 16]))
+
+        def gather_scales(s, tag):
+            e0, e1 = SLICES[s]
+            g_scales[s] = keep.tile([P, (e1 - e0) * C], U8, name="g_scales%d" % s, tag=tag, align_bytes=64)
+            nc.vector.tensor_copy(out=g_scales[s][:], in_=x_scales[:].indirect(offs_sb[:, e0 * C // 16:e1 * C // 16]))
+
+        def interleave_w(c):
+            l0, l1 = W_LOADS[c]
+            for q, (g0, g1) in enumerate(W_BATCHES):
+                lo, hi = max(l0, g0), min(l1, g1)
+                if lo < hi:
+                    copy = nc.vector.tensor_copy if c in VECTOR_LOADS else nc.scalar.copy
+                    copy(
+                        out=w_grp[q][:, lo - g0:hi - g0, :, :].rearrange("p g (c i) j -> p g c j i", i=4),
+                        in_=w_raw[c][:, lo - l0:hi - l0, :].rearrange("p g (j c i) -> p g c j i", j=PACK, i=4),
+                    )
+
+        def weights(q):
+            g0, g1 = W_BATCHES[q]
+            nc.vector.quantize_mx(
+                out=w_codes[q][:].bitcast(FP8X4),
+                scales=w_scales[q][:],
+                in_=w_grp[q][:].rearrange("p g n j -> p (g n j)"),
+            )
+            for g in range(g0, g1):
+                e, a = divmod(g, PASSES)
+                s = find(SLICES, e)
+                k = find(BANKS, e)
+                wc = slice((g - g0) * N, (g - g0 + 1) * N)
+                xc = slice((e - SLICES[s][0]) * C, (e - SLICES[s][0] + 1) * C)
+                nc.tensor.matmul_mx(
+                    out=acc[k][:, e - BANKS[k][0], :],
+                    lhsT=w_codes[q][:, wc].bitcast(FP8X4),
+                    lhsT_scale=w_scales[q][:, wc],
+                    rhs=g_codes[(a, s)][:, xc].bitcast(FP8X4),
+                    rhs_scale=g_scales[s][PACK * a:P, xc],
+                    start=(a == 0),
+                    stop=(a == PASSES - 1),
+                )
+                if a == PASSES - 1 and e + 1 == BANKS[k][1]:
+                    for f in range(BANKS[k][0], BANKS[k][1]):
+                        nc.scalar.activation(out=y[:, f * C:(f + 1) * C], in_=acc[k][:, f - BANKS[k][0], :], func=RELU, bias=b_sb[:, f:f + 1])
+
+        for i, (t0, t1) in enumerate(X_LOADS[0]):
+            cut = (t1 - t0) * V_PART // 8
+            interleave_x(nc.vector.tensor_copy, 0, i, 0, cut)
+            interleave_x(nc.scalar.copy, 0, i, cut, t1 - t0)
+            quantize_x(0, i)
+        for i, (t0, t1) in enumerate(X_LOADS[1]):
+            interleave_x(nc.scalar.copy, 1, i, 0, t1 - t0)
+        for c in range(len(W_LOADS)):
+            interleave_w(c)
+        gather_codes(0, 0, "g_codes00")
+        gather_codes(0, 1, "g_codes01")
+        quantize_x(1, 0)
+        quantize_x(1, 1)
+        gather_codes(1, 0, "g_codes10")
+        gather_scales(0, "g_scales0")
+        gather_codes(1, 1, "g_codes11")
+        gather_scales(1, "g_scales1")
+        for q in range(len(W_BATCHES)):
+            weights(q)
+
+        first = keep.tile([P, T], F32, name="first", tag="raw0")
+        second = keep.tile([P, T], F32, name="second", tag="raw1")
+        total = keep.tile([P, T], F32, name="total", tag="raw2")
+        nc.vector.tensor_tensor(out=first[:], in0=y[:].indirect(pos1_sb[:]), in1=gate_sb[:, 0, :], op=MULT)
+        nc.vector.tensor_tensor(out=second[:], in0=y[:].indirect(pos2_sb[:]), in1=gate_sb[:, 1, :], op=MULT)
+        for h in range(2):
+            cols = slice(h * T // 2, (h + 1) * T // 2)
+            nc.vector.tensor_tensor(out=total[:, cols], in0=first[:, cols], in1=second[:, cols], op=ADD)
+            nc.sync.dma_start(out[:, cols], total[:, cols])

@@ -20,8 +20,8 @@ P = 128
 PACK = 4
 PASSES = K // (P * PACK)
 WINDOW = 2 * T
-X_LOADS = (((0, 512), (512, 768), (768, 1024)), ((0, 512), (512, 1024)))
-X_BATCHES = (((0, 512), (512, 768), (768, 1024)), ((0, 512), (512, 1024)))
+X_LOADS = (((0, 512), (512, 1024)), ((0, 512), (512, 1024)))
+X_BATCHES = (((0, 512), (512, 1024)), ((0, 512), (512, 1024)))
 V_PART = 5
 W_LOADS = ((0, 4), (4, 8), (8, 12), (12, 16), (16, 20), (20, 24), (24, 26), (26, 28), (28, 30), (30, 31), (31, 32))
 W_BATCHES = ((0, 4), (4, 8), (8, 12), (12, 16), (16, 20), (20, 24), (24, 26), (26, 28), (28, 30), (30, 31), (31, 32))
@@ -63,10 +63,11 @@ def tile_routed_moe_kernel(tc, xT, w, b, gate, offs, pos1, pos2, out):
 
         x_view = xT.rearrange("(a p j) t -> a p j t", a=PASSES, p=P, j=PACK)
         w_view = w.rearrange("e (a p j) n -> p (e a) (j n)", a=PASSES, p=P, j=PACK)
-        nc.sync.dma_start(offs_sb[:], offs)
         for a in range(PASSES):
             for i, (t0, t1) in enumerate(X_LOADS[a]):
                 nc.sync.dma_start(x_raw[a][i][:], x_view[a][:, :, t0:t1])
+            if a == 0:
+                nc.sync.dma_start(offs_sb[:], offs)
         for c, (g0, g1) in enumerate(W_LOADS):
             nc.sync.dma_start(w_raw[c][:], w_view[:, g0:g1, :])
             if c == LAST_SCALAR_LOAD:

@@ -20,8 +20,8 @@ P = 128
 PACK = 4
 PASSES = K // (P * PACK)
 WINDOW = 2 * T
-X_LOADS = (((0, 512), (512, 1024)), ((0, 512), (512, 1024)))
-X_BATCHES = (((0, 512), (512, 1024)), ((0, 512), (512, 1024)))
+X_LOADS = (((0, 1024),), ((0, 512), (512, 1024)))
+X_BATCHES = (((0, 256), (256, 512), (512, 768), (768, 1024)), ((0, 512), (512, 1024)))
 V_PART = 5
 W_LOADS = ((0, 4), (4, 8), (8, 12), (12, 16), (16, 20), (20, 24), (24, 26), (26, 28), (28, 30), (30, 31), (31, 32))
 W_BATCHES = ((0, 4), (4, 8), (8, 12), (12, 16), (16, 20), (20, 24), (24, 26), (26, 28), (28, 30), (30, 31), (31, 32))
@@ -145,11 +145,11 @@ def tile_routed_moe_kernel(tc, xT, w, b, gate, offs, pos1, pos2, out):
                     for f in range(BANKS[k][0], BANKS[k][1]):
                         nc.scalar.activation(out=y[:, f * C:(f + 1) * C], in_=acc[k][:, f - BANKS[k][0], :], func=RELU, bias=b_sb[:, f:f + 1])
 
-        for i, (t0, t1) in enumerate(X_LOADS[0]):
-            cut = (t1 - t0) * V_PART // 8
-            interleave_x(nc.vector.tensor_copy, 0, i, 0, cut)
-            interleave_x(nc.scalar.copy, 0, i, cut, t1 - t0)
-            quantize_x(0, i)
+        for q, (t0, t1) in enumerate(X_BATCHES[0]):
+            cut = t0 + (t1 - t0) * V_PART // 8
+            interleave_x(nc.vector.tensor_copy, 0, 0, t0, cut)
+            interleave_x(nc.scalar.copy, 0, 0, cut, t1)
+            quantize_x(0, q)
         for i, (t0, t1) in enumerate(X_LOADS[1]):
             interleave_x(nc.scalar.copy, 1, i, 0, t1 - t0)
         for c in range(len(W_LOADS)):

@@ -26,8 +26,8 @@ V_PART = 5
 W_LOADS = ((0, 4), (4, 8), (8, 12), (12, 16), (16, 20), (20, 24), (24, 26), (26, 28), (28, 30), (30, 31), (31, 32))
 W_BATCHES = ((0, 4), (4, 8), (8, 12), (12, 16), (16, 20), (20, 24), (24, 26), (26, 28), (28, 30), (30, 31), (31, 32))
 SLICES = ((0, 12), (12, 16))
-VECTOR_LOADS = (7, 8, 9, 10)
-LAST_SCALAR_LOAD = 6
+VECTOR_LOADS = (8, 9, 10)
+LAST_SCALAR_LOAD = 7
 BANKS = ((0, 4), (4, 6), (6, 8), (8, 10), (10, 12), (12, 14), (14, 15), (15, 16))
 
 

@@ -28,6 +28,7 @@ W_BATCHES = ((0, 4), (4, 8), (8, 12), (12, 16), (16, 20), (20, 24), (24, 26), (2
 SLICES = ((0, 12), (12, 16))
 VECTOR_LOADS = (8, 9, 10)
 LAST_SCALAR_LOAD = 7
+GPSIMD_LOADS = (1,)
 BANKS = ((0, 4), (4, 6), (6, 8), (8, 10), (10, 12), (12, 14), (14, 15), (15, 16))
 
 
@@ -112,7 +113,17 @@ def tile_routed_moe_kernel(tc, xT, w, b, gate, offs, pos1, pos2, out):
             l0, l1 = W_LOADS[c]
             for q, (g0, g1) in enumerate(W_BATCHES):
                 lo, hi = max(l0, g0), min(l1, g1)
-                if lo < hi:
+                if lo < hi and c in GPSIMD_LOADS:
+                    for g in range(lo, hi):
+                        nc.gpsimd.tensor_scalar(
+                            out=w_grp[q][:, g - g0, :, :],
+                            in0=w_raw[c][:, g - l0, :].rearrange("p (j n) -> p n j", j=PACK),
+                            scalar1=1.0,
+                            scalar2=0.0,
+                            op0=MULT,
+                            op1=ADD,
+                        )
+                elif lo < hi:
                     copy = nc.vector.tensor_copy if c in VECTOR_LOADS else nc.scalar.copy
                     copy(
                         out=w_grp[q][:, lo - g0:hi - g0, :, :].rearrange("p g (c i) j -> p g c j i", i=4),

@@ -20,7 +20,7 @@ P = 128
 PACK = 4
 PASSES = K // (P * PACK)
 WINDOW = 2 * T
-X_LOADS = (((0, 1024),), ((0, 512), (512, 1024)))
+X_LOADS = (((0, 1024),), ((0, 1024),))
 X_BATCHES = (((0, 256), (256, 512), (512, 768), (768, 1024)), ((0, 512), (512, 1024)))
 V_PART = 5
 W_LOADS = ((0, 4), (4, 8), (8, 12), (12, 16), (16, 20), (20, 24), (24, 26), (26, 28), (28, 30), (30, 31), (31, 32))
@@ -161,8 +161,9 @@ def tile_routed_moe_kernel(tc, xT, w, b, gate, offs, pos1, pos2, out):
             interleave_x(nc.vector.tensor_copy, 0, 0, t0, cut)
             interleave_x(nc.scalar.copy, 0, 0, cut, t1)
             quantize_x(0, q)
-        for i, (t0, t1) in enumerate(X_LOADS[1]):
-            interleave_x(nc.scalar.copy, 1, i, 0, t1 - t0)
+        interleave_x(nc.scalar.copy, 1, 0, 0, 512)
+        interleave_x(nc.scalar.copy, 1, 0, 512, 768)
+        interleave_x(nc.vector.tensor_copy, 1, 0, 768, 1024)
         for c in range(len(W_LOADS)):
             interleave_w(c)
         gather_codes(0, 0, "g_codes00")

@@ -23,12 +23,12 @@ WINDOW = 2 * T
 X_LOADS = (((0, 1024),), ((0, 1024),))
 X_BATCHES = (((0, 256), (256, 512), (512, 768), (768, 1024)), ((0, 512), (512, 1024)))
 V_PART = 5
-W_LOADS = ((0, 4), (4, 8), (8, 12), (12, 16), (16, 20), (20, 24), (24, 26), (26, 28), (28, 30), (30, 31), (31, 32))
+W_LOADS = ((0, 4), (4, 8), (8, 12), (12, 14), (14, 16), (16, 18), (18, 20), (20, 22), (22, 24), (24, 26), (26, 28), (28, 30), (30, 31), (31, 32))
 W_BATCHES = ((0, 4), (4, 8), (8, 12), (12, 16), (16, 20), (20, 24), (24, 26), (26, 28), (28, 30), (30, 31), (31, 32))
 SLICES = ((0, 12), (12, 16))
-VECTOR_LOADS = (8, 9, 10)
-LAST_SCALAR_LOAD = 7
-GPSIMD_LOADS = (1,)
+VECTOR_LOADS = (11, 12, 13)
+LAST_SCALAR_LOAD = 10
+GPSIMD_LOADS = (1, 3)
 BANKS = ((0, 4), (4, 6), (6, 8), (8, 10), (10, 12), (12, 14), (14, 15), (15, 16))
 
 

@@ -17,6 +17,7 @@ ADD = mybir.AluOpType.add
 RELU = mybir.ActivationFunctionType.Relu
 
 P = 128
+DMA_ALIGN = 256
 PACK = 4
 PASSES = K // (P * PACK)
 WINDOW = 2 * T
@@ -26,8 +27,8 @@ V_PART = 5
 W_LOADS = ((0, 4), (4, 8), (8, 12), (12, 14), (14, 16), (16, 18), (18, 20), (20, 22), (22, 24), (24, 26), (26, 28), (28, 30), (30, 31), (31, 32))
 W_BATCHES = ((0, 4), (4, 8), (8, 12), (12, 16), (16, 20), (20, 24), (24, 26), (26, 28), (28, 30), (30, 31), (31, 32))
 SLICES = ((0, 12), (12, 16))
-VECTOR_LOADS = (11, 12, 13)
-LAST_SCALAR_LOAD = 10
+VECTOR_LOADS = (12, 13)
+LAST_SCALAR_LOAD = 11
 GPSIMD_LOADS = (1, 3)
 BANKS = ((0, 4), (4, 6), (6, 8), (8, 10), (10, 12), (12, 14), (14, 15), (15, 16))
 
@@ -47,16 +48,16 @@ def tile_routed_moe_kernel(tc, xT, w, b, gate, offs, pos1, pos2, out):
         pos1_sb = lists.tile([P, T // 16], U16, name="pos1_sb")
         pos2_sb = lists.tile([P, T // 16], U16, name="pos2_sb")
 
-        x_raw = [[keep.tile([P, PACK, t1 - t0], F32, name="x_raw%d%d" % (a, i)) for i, (t0, t1) in enumerate(X_LOADS[a])] for a in range(PASSES)]
+        x_raw = [[keep.tile([P, PACK, t1 - t0], F32, name="x_raw%d%d" % (a, i), align_bytes=DMA_ALIGN) for i, (t0, t1) in enumerate(X_LOADS[a])] for a in range(PASSES)]
         x_grp = [[keep.tile([P, t1 - t0, PACK], BF16, name="x_grp%d%d" % (a, i), align_bytes=64) for i, (t0, t1) in enumerate(X_BATCHES[a])] for a in range(PASSES)]
         x_codes = [keep.tile([P, WINDOW], I32, name="x_codes%d" % a, align_bytes=64) for a in range(PASSES)]
         x_scales = keep.tile([P, WINDOW], U8, name="x_scales", align_bytes=64)
-        w_raw = [keep.tile([P, g1 - g0, PACK * N], F32, name="w_raw%d" % c, tag="raw%d" % c) for c, (g0, g1) in enumerate(W_LOADS)]
+        w_raw = [keep.tile([P, g1 - g0, PACK * N], F32, name="w_raw%d" % c, tag="raw%d" % c, align_bytes=DMA_ALIGN) for c, (g0, g1) in enumerate(W_LOADS)]
         w_grp = [keep.tile([P, g1 - g0, N, PACK], BF16, name="w_grp%d" % q, tag="slot%d" % q, align_bytes=64) for q, (g0, g1) in enumerate(W_BATCHES)]
         w_codes = [keep.tile([P, (g1 - g0) * N], U32, name="w_codes%d" % q, align_bytes=64) for q, (g0, g1) in enumerate(W_BATCHES)]
         w_scales = [keep.tile([P, (g1 - g0) * N], U8, name="w_scales%d" % q, align_bytes=64) for q, (g0, g1) in enumerate(W_BATCHES)]
         b_sb = keep.tile([P, E], F32, name="b_sb")
-        gate_sb = keep.tile([P, 2, T], F32, name="gate_sb")
+        gate_sb = keep.tile([P, 2, T], F32, name="gate_sb", align_bytes=DMA_ALIGN)
         y = keep.tile([P, E * C], F32, name="y")
         acc = [psum.tile([N, e1 - e0, C], F32, name="acc%d" % k) for k, (e0, e1) in enumerate(BANKS)]
         g_codes = {}
@@ -162,8 +163,8 @@ def tile_routed_moe_kernel(tc, xT, w, b, gate, offs, pos1, pos2, out):
             interleave_x(nc.scalar.copy, 0, 0, cut, t1)
             quantize_x(0, q)
         interleave_x(nc.scalar.copy, 1, 0, 0, 512)
-        interleave_x(nc.scalar.copy, 1, 0, 512, 768)
-        interleave_x(nc.vector.tensor_copy, 1, 0, 768, 1024)
+        interleave_x(nc.scalar.copy, 1, 0, 512, 832)
+        interleave_x(nc.vector.tensor_copy, 1, 0, 832, 1024)
         for c in range(len(W_LOADS)):
             interleave_w(c)
         gather_codes(0, 0, "g_codes00")
@@ -177,9 +178,9 @@ def tile_routed_moe_kernel(tc, xT, w, b, gate, offs, pos1, pos2, out):
         for q in range(len(W_BATCHES)):
             weights(q)
 
-        first = keep.tile([P, T], F32, name="first", tag="raw0")
-        second = keep.tile([P, T], F32, name="second", tag="raw1")
-        total = keep.tile([P, T], F32, name="total", tag="raw2")
+        first = keep.tile([P, T], F32, name="first", tag="raw0", align_bytes=DMA_ALIGN)
+        second = keep.tile([P, T], F32, name="second", tag="raw1", align_bytes=DMA_ALIGN)
+        total = keep.tile([P, T], F32, name="total", tag="raw2", align_bytes=DMA_ALIGN)
         nc.vector.tensor_tensor(out=first[:], in0=y[:].indirect(pos1_sb[:]), in1=gate_sb[:, 0, :], op=MULT)
         nc.vector.tensor_tensor(out=second[:], in0=y[:].indirect(pos2_sb[:]), in1=gate_sb[:, 1, :], op=MULT)
         for h in range(2):

from contextlib import ExitStack

import concourse.mybir as mybir

K, T, E, C, N = 1024, 1024, 16, 128, 128
FLOPS = 2 * K * N * E * C

F32 = mybir.dt.float32
BF16 = mybir.dt.bfloat16
U32 = mybir.dt.uint32
I32 = mybir.dt.int32
U16 = mybir.dt.uint16
U8 = mybir.dt.uint8
FP8X4 = mybir.dt.float8_e4m3fn_x4
MULT = mybir.AluOpType.mult
ADD = mybir.AluOpType.add
RELU = mybir.ActivationFunctionType.Relu

P = 128
DMA_ALIGN = 256
PACK = 4
PASSES = K // (P * PACK)
WINDOW = 2 * T
X_LOADS = (((0, 1024),), ((0, 1024),))
X_BATCHES = (((0, 256), (256, 512), (512, 768), (768, 1024)), ((0, 512), (512, 1024)))
V_PART = 5
W_LOADS = ((0, 4), (4, 8), (8, 12), (12, 14), (14, 16), (16, 18), (18, 20), (20, 22), (22, 24), (24, 26), (26, 28), (28, 30), (30, 31), (31, 32))
W_BATCHES = ((0, 4), (4, 8), (8, 12), (12, 16), (16, 20), (20, 24), (24, 26), (26, 28), (28, 30), (30, 31), (31, 32))
SLICES = ((0, 12), (12, 16))
VECTOR_LOADS = (12, 13)
LAST_SCALAR_LOAD = 11
GPSIMD_LOADS = (1, 3)
BANKS = ((0, 4), (4, 6), (6, 8), (8, 10), (10, 12), (12, 14), (14, 15), (15, 16))


def find(ranges, i):
    return [k for k, (r0, r1) in enumerate(ranges) if r0 <= i < r1][0]


def tile_routed_moe_kernel(tc, xT, w, b, gate, offs, pos1, pos2, out):
    nc = tc.nc
    with ExitStack() as ctx:
        lists = ctx.enter_context(tc.tile_pool(name="lists", bufs=1))
        keep = ctx.enter_context(tc.tile_pool(name="keep", bufs=1))
        psum = ctx.enter_context(tc.psum_pool(name="psum", bufs=1))

        offs_sb = lists.tile([P, E * C // 16], U16, name="offs_sb")
        pos1_sb = lists.tile([P, T // 16], U16, name="pos1_sb")
        pos2_sb = lists.tile([P, T // 16], U16, name="pos2_sb")

        x_raw = [[keep.tile([P, PACK, t1 - t0], F32, name="x_raw%d%d" % (a, i), align_bytes=DMA_ALIGN) for i, (t0, t1) in enumerate(X_LOADS[a])] for a in range(PASSES)]
        x_grp = [[keep.tile([P, t1 - t0, PACK], BF16, name="x_grp%d%d" % (a, i), align_bytes=64) for i, (t0, t1) in enumerate(X_BATCHES[a])] for a in range(PASSES)]
        x_codes = [keep.tile([P, WINDOW], I32, name="x_codes%d" % a, align_bytes=64) for a in range(PASSES)]
        x_scales = keep.tile([P, WINDOW], U8, name="x_scales", align_bytes=64)
        w_raw = [keep.tile([P, g1 - g0, PACK * N], F32, name="w_raw%d" % c, tag="raw%d" % c, align_bytes=DMA_ALIGN) for c, (g0, g1) in enumerate(W_LOADS)]
        w_grp = [keep.tile([P, g1 - g0, N, PACK], BF16, name="w_grp%d" % q, tag="slot%d" % q, align_bytes=64) for q, (g0, g1) in enumerate(W_BATCHES)]
        w_codes = [keep.tile([P, (g1 - g0) * N], U32, name="w_codes%d" % q, align_bytes=64) for q, (g0, g1) in enumerate(W_BATCHES)]
        w_scales = [keep.tile([P, (g1 - g0) * N], U8, name="w_scales%d" % q, align_bytes=64) for q, (g0, g1) in enumerate(W_BATCHES)]
        b_sb = keep.tile([P, E], F32, name="b_sb")
        gate_sb = keep.tile([P, 2, T], F32, name="gate_sb", align_bytes=DMA_ALIGN)
        y = keep.tile([P, E * C], F32, name="y")
        acc = [psum.tile([N, e1 - e0, C], F32, name="acc%d" % k) for k, (e0, e1) in enumerate(BANKS)]
        g_codes = {}
        g_scales = {}

        x_view = xT.rearrange("(a p j) t -> a p j t", a=PASSES, p=P, j=PACK)
        w_view = w.rearrange("e (a p j) n -> p (e a) (j n)", a=PASSES, p=P, j=PACK)
        for a in range(PASSES):
            for i, (t0, t1) in enumerate(X_LOADS[a]):
                nc.sync.dma_start(x_raw[a][i][:], x_view[a][:, :, t0:t1])
            if a == 0:
                nc.sync.dma_start(offs_sb[:], offs)
        for c, (g0, g1) in enumerate(W_LOADS):
            nc.sync.dma_start(w_raw[c][:], w_view[:, g0:g1, :])
            if c == LAST_SCALAR_LOAD:
                nc.sync.dma_start(b_sb[:], b)
        nc.sync.dma_start(pos1_sb[:], pos1)
        nc.sync.dma_start(pos2_sb[:], pos2)
        for g in range(2):
            nc.sync.dma_start(gate_sb[:, g, :], gate[g])

        nc.vector.memset(x_scales[:].bitcast(I32), 0)
        for a in range(PASSES):
            nc.vector.memset(x_codes[a][:, T:WINDOW], 0)

        def interleave_x(copy, a, i, t0, t1):
            base = X_LOADS[a][i][0]
            q = find(X_BATCHES[a], base + t0)
            shift = base - X_BATCHES[a][q][0]
            copy(
                out=x_grp[a][q][:, shift + t0:shift + t1, :].rearrange("p (c i) j -> p c j i", i=4),
                in_=x_raw[a][i][:, :, t0:t1].rearrange("p j (c i) -> p c j i", i=4),
            )

        def quantize_x(a, q):
            t0, t1 = X_BATCHES[a][q]
            nc.vector.quantize_mx(
                out=x_codes[a][:, t0:t1].bitcast(FP8X4),
                scales=x_scales[PACK * a:P, t0:t1],
                in_=x_grp[a][q][:].rearrange("p t j -> p (t j)"),
            )

        def gather_codes(a, s, tag):
            e0, e1 = SLICES[s]
            g_codes[(a, s)] = keep.tile([P, (e1 - e0) * C], U32, name="g_codes%d%d" % (a, s), tag=tag, align_bytes=64)
            nc.vector.tensor_copy(out=g_codes[(a, s)][:], in_=x_codes[a][:].bitcast(U32).indirect(offs_sb[:, e0 * C // 16:e1 * C // 16]))

        def gather_scales(s, tag):
            e0, e1 = SLICES[s]
            g_scales[s] = keep.tile([P, (e1 - e0) * C], U8, name="g_scales%d" % s, tag=tag, align_bytes=64)
            nc.vector.tensor_copy(out=g_scales[s][:], in_=x_scales[:].indirect(offs_sb[:, e0 * C // 16:e1 * C // 16]))

        def interleave_w(c):
            l0, l1 = W_LOADS[c]
            for q, (g0, g1) in enumerate(W_BATCHES):
                lo, hi = max(l0, g0), min(l1, g1)
                if lo < hi and c in GPSIMD_LOADS:
                    for g in range(lo, hi):
                        nc.gpsimd.tensor_scalar(
                            out=w_grp[q][:, g - g0, :, :],
                            in0=w_raw[c][:, g - l0, :].rearrange("p (j n) -> p n j", j=PACK),
                            scalar1=1.0,
                            scalar2=0.0,
                            op0=MULT,
                            op1=ADD,
                        )
                elif lo < hi:
                    copy = nc.vector.tensor_copy if c in VECTOR_LOADS else nc.scalar.copy
                    copy(
                        out=w_grp[q][:, lo - g0:hi - g0, :, :].rearrange("p g (c i) j -> p g c j i", i=4),
                        in_=w_raw[c][:, lo - l0:hi - l0, :].rearrange("p g (j c i) -> p g c j i", j=PACK, i=4),
                    )

        def weights(q):
            g0, g1 = W_BATCHES[q]
            nc.vector.quantize_mx(
                out=w_codes[q][:].bitcast(FP8X4),
                scales=w_scales[q][:],
                in_=w_grp[q][:].rearrange("p g n j -> p (g n j)"),
            )
            for g in range(g0, g1):
                e, a = divmod(g, PASSES)
                s = find(SLICES, e)
                k = find(BANKS, e)
                wc = slice((g - g0) * N, (g - g0 + 1) * N)
                xc = slice((e - SLICES[s][0]) * C, (e - SLICES[s][0] + 1) * C)
                nc.tensor.matmul_mx(
                    out=acc[k][:, e - BANKS[k][0], :],
                    lhsT=w_codes[q][:, wc].bitcast(FP8X4),
                    lhsT_scale=w_scales[q][:, wc],
                    rhs=g_codes[(a, s)][:, xc].bitcast(FP8X4),
                    rhs_scale=g_scales[s][PACK * a:P, xc],
                    start=(a == 0),
                    stop=(a == PASSES - 1),
                )
                if a == PASSES - 1 and e + 1 == BANKS[k][1]:
                    for f in range(BANKS[k][0], BANKS[k][1]):
                        nc.scalar.activation(out=y[:, f * C:(f + 1) * C], in_=acc[k][:, f - BANKS[k][0], :], func=RELU, bias=b_sb[:, f:f + 1])

        for q, (t0, t1) in enumerate(X_BATCHES[0]):
            cut = t0 + (t1 - t0) * V_PART // 8
            interleave_x(nc.vector.tensor_copy, 0, 0, t0, cut)
            interleave_x(nc.scalar.copy, 0, 0, cut, t1)
            quantize_x(0, q)
        interleave_x(nc.scalar.copy, 1, 0, 0, 512)
        interleave_x(nc.scalar.copy, 1, 0, 512, 832)
        interleave_x(nc.vector.tensor_copy, 1, 0, 832, 1024)
        for c in range(len(W_LOADS)):
            interleave_w(c)
        gather_codes(0, 0, "g_codes00")
        gather_codes(0, 1, "g_codes01")
        quantize_x(1, 0)
        quantize_x(1, 1)
        gather_codes(1, 0, "g_codes10")
        gather_scales(0, "g_scales0")
        gather_codes(1, 1, "g_codes11")
        gather_scales(1, "g_scales1")
        for q in range(len(W_BATCHES)):
            weights(q)

        first = keep.tile([P, T], F32, name="first", tag="raw0", align_bytes=DMA_ALIGN)
        second = keep.tile([P, T], F32, name="second", tag="raw1", align_bytes=DMA_ALIGN)
        total = keep.tile([P, T], F32, name="total", tag="raw2", align_bytes=DMA_ALIGN)
        nc.vector.tensor_tensor(out=first[:], in0=y[:].indirect(pos1_sb[:]), in1=gate_sb[:, 0, :], op=MULT)
        nc.vector.tensor_tensor(out=second[:], in0=y[:].indirect(pos2_sb[:]), in1=gate_sb[:, 1, :], op=MULT)
        for h in range(2):
            cols = slice(h * T // 2, (h + 1) * T // 2)
            nc.vector.tensor_tensor(out=total[:, cols], in0=first[:, cols], in1=second[:, cols], op=ADD)
            nc.sync.dma_start(out[:, cols], total[:, cols])
